import numpy as np
import ml_dtypes


def mxq(x, axis, fmt="e4m3"):
    dtype, down = {"e4m3": (ml_dtypes.float8_e4m3fn, 7), "e5m2": (ml_dtypes.float8_e5m2, 14)}[fmt]
    v = np.moveaxis(np.asarray(x, np.float32).astype(ml_dtypes.bfloat16).astype(np.float64), axis, -1)
    blocks = v.reshape(v.shape[:-1] + (-1, 32))
    amax = np.abs(blocks).max(-1, keepdims=True)
    byte = np.maximum(np.where(amax > 0, np.frexp(amax)[1] - 1 + 127, 0) - down, 1)
    scale = np.exp2(byte - 127.0)
    codes = (blocks / scale).astype(np.float32).astype(dtype).astype(np.float64)
    return np.moveaxis((codes * scale).reshape(v.shape), -1, axis)


WIDE = False


def mx_kscale(k):
    if not WIDE:
        return np.ones(k)
    levels = np.array([10, -10, 5, -5, 0])
    if k % 512:
        return np.exp2(np.random.permutation(np.resize(levels, k // 32))).repeat(32)
    a = np.empty((k // 512, 16))
    for p in range(k // 512):
        a[p, :8] = np.random.permutation(np.resize(levels, 8))
        for g in range(8):
            far = levels[np.abs(levels - a[p, g]) >= 10]
            a[p, g + 8] = far[np.random.randint(len(far))]
    return np.exp2(a.ravel()).repeat(32)


def f64(x):
    return np.asarray(x).astype(np.float64)


def striped(idx):
    return np.tile(np.asarray(idx).reshape(-1, 16).T, (8, 1)).astype(np.uint16)


def unstriped(offs):
    return offs[:16].T.reshape(-1).astype(np.int64)


E2M1 = np.array([0.0, 0.5, 1.0, 1.5, 2.0, 3.0, 4.0, 6.0, -0.0, -0.5, -1.0, -1.5, -2.0, -3.0, -4.0, -6.0])


def pack_weight(w, fmt):
    k, n = w.shape
    w = f64(np.asarray(w, np.float32).astype(ml_dtypes.bfloat16)).reshape(k // 32, 32, n)
    amax = np.abs(w).max(1)
    if fmt == "e4m3":
        byte = np.frexp(amax)[1] - 1 + 127 - 7
    else:
        mant, ex = np.frexp(amax / 6.0)
        byte = np.where(mant > 0.5, ex, ex - 1) + 127
    byte = np.clip(np.where(amax > 0, byte, 1), 1, 254)
    scaled = (w * np.exp2(127.0 - byte)[:, None, :]).reshape(k, n).astype(np.float32)
    by_word = np.ascontiguousarray(scaled.reshape(k // 512, 128, 4, n).transpose(0, 1, 3, 2))
    if fmt == "e4m3":
        words = by_word.astype(ml_dtypes.float8_e4m3fn).view(np.uint8)
    else:
        c = by_word.astype(ml_dtypes.float4_e2m1fn).view(np.uint8) & 0xF
        words = (c[..., 0::2] | (c[..., 1::2] << 4)).reshape(k // 512, 128, 2 * n)
    return np.ascontiguousarray(words), np.ascontiguousarray(byte.astype(np.uint8).reshape(k // 512, 16, n))


def unpack_weight(words, scales, fmt):
    g, _, n = scales.shape
    words = np.ascontiguousarray(words).reshape(g, 128, n, -1)
    if fmt == "e4m3":
        vals = words.view(ml_dtypes.float8_e4m3fn).astype(np.float64)
    else:
        nib = np.empty((g, 128, n, 4), np.uint8)
        nib[..., 0::2] = words & 0xF
        nib[..., 1::2] = words >> 4
        vals = E2M1[nib]
    vals = vals * np.repeat(np.exp2(scales.astype(np.float64) - 127.0), 8, axis=1)[..., None]
    return vals.transpose(0, 1, 3, 2).reshape(g * 512, n)


B, N, T, D, NQ = 2, 512, 2048, 1024, 128


def setup_inputs():
    n = np.random.standard_normal
    jdx = np.random.permutation(1024)[:B * NQ]
    pages = np.random.permutation(T // 32)[:B * N // 32]
    idx = (pages[:, None] * 32 + np.arange(32)[None, :]).reshape(-1)
    s = mx_kscale(D)[:, None]
    kp = pack_weight(n((D, T)) / s, "e2m1")
    return {
        "qT": (n((D, 1024)) * s * (1.00 / np.sqrt(D))).astype(np.float32),
        "k_words": np.ascontiguousarray(kp[0].reshape(1, 2, 128, T, 2).transpose(0, 2, 3, 1, 4)).reshape(1, 128, T, 4),
        "k_scales": kp[1],
        "offq": striped(jdx),
        "offs": striped(idx),
    }


def reference(qT, k_words, k_scales, offq, offs):
    jdx = unstriped(offq)
    idx = unstriped(offs)
    pick = lambda x, which: x[:, which].reshape(x.shape[0], B, -1).transpose(1, 0, 2)
    qg = mxq(pick(f64(qT), jdx), 1, "e4m3")
    k = unpack_weight(k_words.reshape(1, 128, T, 2, 2).transpose(0, 3, 1, 2, 4).reshape(2, 128, 2 * T), k_scales, "e2m1")
    kg = pick(k, idx)
    qq = qg
    a = qq.transpose(0, 2, 1) @ kg
    m = np.max(a, axis=-1, keepdims=True)
    e = np.exp(a - m)
    l = np.sum(e, axis=-1, keepdims=True)
    y = e / l
    return y

@@ -1,0 +1,139 @@
+from contextlib import ExitStack
+
+import concourse.mybir as mybir
+
+B, N, T, D, NQ, POOL = 2, 512, 2048, 1024, 128, 1024
+FLOPS = 2 * B * NQ * N * D
+
+F32 = mybir.dt.float32
+BF16 = mybir.dt.bfloat16
+I32 = mybir.dt.int32
+U32 = mybir.dt.uint32
+U16 = mybir.dt.uint16
+U8 = mybir.dt.uint8
+FP8X4 = mybir.dt.float8_e4m3fn_x4
+FP4X4 = mybir.dt.float4_e2m1fn_x4
+ACT = mybir.ActivationFunctionType
+ALU = mybir.AluOpType
+AX = mybir.AxisListType
+
+P = 128
+PACK = 4
+PASSES = D // (P * PACK)
+SHIFT = 16
+
+
+def tile_attend_lq_wts_kernel(tc, qT, k_words, k_scales, offq, offs, out):
+    nc = tc.nc
+    with ExitStack() as ctx:
+        keep = ctx.enter_context(tc.tile_pool(name="keep", bufs=1))
+        psum = ctx.enter_context(tc.psum_pool(name="psum", bufs=1))
+
+        key_list = keep.tile([P, B * N // 16], U16, name="key_list")
+        query_list = keep.tile([P, B * NQ // 16], U16, name="query_list")
+        word_pool = keep.tile([P, T], I32, name="word_pool")
+        scale_pool = keep.tile([P, T], U8, name="scale_pool")
+        scale_late = keep.tile([P, B * N], U8, name="scale_late", align_bytes=64)
+
+        warm = keep.tile([P, 1], F32, name="warm")
+        warmed = keep.tile([P, 1], F32, name="warmed")
+        nc.vector.memset(scale_pool[:].bitcast(I32), 0)
+        nc.vector.memset(warm[:], 0.0)
+        nc.vector.memset(scale_late[:].bitcast(I32), 0)
+
+        nc.sync.dma_start(key_list[:], offs)
+        nc.sync.dma_start(word_pool[:], k_words[0].rearrange("p t c -> p (t c)").bitcast(I32))
+
+        scale_rows = k_scales.rearrange("o (q r) t -> r q o t", r=4)
+        for r in range(4):
+            nc.scalar.dma_start(scale_pool[r:P:SHIFT, :].bitcast(I32), scale_rows[r].bitcast(I32))
+        nc.scalar.activation(warmed[:], warm[:], ACT.Exp)
+        nc.sync.dma_start(query_list[:], offq)
+
+        q_rows = qT.rearrange("(o p j) w -> o p j w", o=PASSES, j=PACK)
+        pairs = []
+        for h in range(2):
+            pair = keep.tile([P, 2, POOL], F32, name=f"pair{h}")
+            nc.sync.dma_start(pair[:], q_rows[0][:, 2 * h : 2 * h + 2, :])
+            pairs.append(pair)
+        rows = []
+        for j in range(PACK):
+            row = keep.tile([P, POOL], F32, name=f"row{j}")
+            nc.sync.dma_start(row[:], q_rows[1][:, j, :])
+            rows.append(row)
+
+        scale_listed = keep.tile([P, B * N], U8, name="scale_listed", align_bytes=64)
+        nc.vector.tensor_copy(scale_listed[:], scale_pool[:].indirect(key_list[:]))
+        nc.sync.dma_start(scale_late[0 : P - SHIFT, :].bitcast(I32), scale_listed[SHIFT:P, :].bitcast(I32))
+        words_listed = keep.tile([P, B * N], U32, name="words_listed")
+        nc.vector.tensor_copy(words_listed[:], word_pool[:].bitcast(U32).indirect(key_list[:]))
+        halves = words_listed[:].bitcast(U16).rearrange("p (n h) -> p h n", h=2)
+        key_codes = []
+        for o in range(PASSES):
+            codes = keep.tile([P, B * N], U16, name=f"key_codes{o}", align_bytes=64)
+            nc.vector.tensor_copy(codes[:], halves[:, o, :])
+            key_codes.append(codes)
+        key_scales = [scale_listed, scale_late]
+
+        woven = [keep.tile([P, B * NQ, PACK], BF16, name=f"woven{o}", align_bytes=64) for o in range(PASSES)]
+        q_codes = [keep.tile([P, B * NQ], U32, name=f"q_codes{o}", align_bytes=64) for o in range(PASSES)]
+        q_scales = [keep.tile([P, B * NQ], U8, name=f"q_scales{o}", align_bytes=64) for o in range(PASSES)]
+        woven_words = woven[0][:].rearrange("p n j -> p (n j)").bitcast(U32).rearrange("p (n h) -> p n h", h=2)
+        for h in range(2):
+            cast = keep.tile([P, POOL, 2], BF16, name=f"cast{h}")
+            nc.scalar.activation(cast[:], pairs[h][:].rearrange("p j w -> p w j"), ACT.Copy)
+            window = cast[:].rearrange("p w j -> p (w j)").bitcast(U32)
+            nc.vector.tensor_copy(woven_words[:, :, h], window.indirect(query_list[:]))
+        nc.vector.quantize_mx(
+            out=q_codes[0][:].bitcast(FP8X4),
+            scales=q_scales[0][:],
+            in_=woven[0][:].rearrange("p n j -> p (n j)"),
+        )
+
+        scores = [psum.tile([P, N], F32, name=f"scores{b}") for b in range(B)]
+
+        def multiply(b, o):
+            qs = slice(b * NQ, (b + 1) * NQ)
+            ks = slice(b * N, (b + 1) * N)
+            nc.tensor.matmul_mx(
+                out=scores[b][:],
+                lhsT=q_codes[o][:, qs].bitcast(FP8X4),
+                lhsT_scale=q_scales[o][:, qs],
+                rhs=key_codes[o][:, ks].bitcast(FP4X4),
+                rhs_scale=key_scales[o][:, ks],
+                start=(o == 0),
+                stop=(o == PASSES - 1),
+            )
+
+        for b in range(B):
+            multiply(b, 0)
+
+        for j in range(PACK - 1):
+            nc.vector.tensor_copy(woven[1][:, :, j], rows[j][:].indirect(query_list[:]))
+        cols = NQ // 16
+        for b in range(B):
+            nc.vector.tensor_copy(
+                woven[1][:, b * NQ : (b + 1) * NQ, PACK - 1],
+                rows[PACK - 1][:].indirect(query_list[:, b * cols : (b + 1) * cols]),
+            )
+        for b in range(B):
+            qs = slice(b * NQ, (b + 1) * NQ)
+            nc.vector.quantize_mx(
+                out=q_codes[1][:, qs].bitcast(FP8X4),
+                scales=q_scales[1][:, qs],
+                in_=woven[1][:, qs, :].rearrange("p n j -> p (n j)"),
+            )
+            multiply(b, 1)
+
+        neg_max = [keep.tile([P, 1], F32, name=f"neg_max{b}") for b in range(B)]
+        total = [keep.tile([P, 1], F32, name=f"total{b}") for b in range(B)]
+        inverse = [keep.tile([P, 1], F32, name=f"inverse{b}") for b in range(B)]
+        weights = [keep.tile([P, N], F32, name=f"weights{b}") for b in range(B)]
+        result = [keep.tile([P, N], F32, name=f"result{b}") for b in range(B)]
+        for b in range(B):
+            nc.vector.tensor_reduce(neg_max[b][:], scores[b][:], AX.X, ALU.max, negate=True)
+            nc.scalar.activation(weights[b][:], scores[b][:], ACT.Exp, bias=neg_max[b][:], scale=1.0, accum_out=total[b][:])
+        for b in range(B):
+            nc.vector.reciprocal(inverse[b][:], total[b][:])
+            nc.vector.tensor_scalar_mul(result[b][:], weights[b][:], inverse[b][:])
+            nc.sync.dma_start(out[b], result[b][:])

@@ -35,10 +35,7 @@ def tile_attend_lq_wts_kernel(tc, qT, k_words, k_scales, offq, offs, out):
         scale_pool = keep.tile([P, T], U8, name="scale_pool")
         scale_late = keep.tile([P, B * N], U8, name="scale_late", align_bytes=64)
 
-        warm = keep.tile([P, 1], F32, name="warm")
-        warmed = keep.tile([P, 1], F32, name="warmed")
         nc.vector.memset(scale_pool[:].bitcast(I32), 0)
-        nc.vector.memset(warm[:], 0.0)
         nc.vector.memset(scale_late[:].bitcast(I32), 0)
 
         nc.sync.dma_start(key_list[:], offs)
@@ -47,20 +44,15 @@ def tile_attend_lq_wts_kernel(tc, qT, k_words, k_scales, offq, offs, out):
         scale_rows = k_scales.rearrange("o (q r) t -> r q o t", r=4)
         for r in range(4):
             nc.scalar.dma_start(scale_pool[r:P:SHIFT, :].bitcast(I32), scale_rows[r].bitcast(I32))
-        nc.scalar.activation(warmed[:], warm[:], ACT.Exp)
         nc.sync.dma_start(query_list[:], offq)
 
         q_rows = qT.rearrange("(o p j) w -> o p j w", o=PASSES, j=PACK)
-        pairs = []
-        for h in range(2):
-            pair = keep.tile([P, 2, POOL], F32, name=f"pair{h}")
-            nc.sync.dma_start(pair[:], q_rows[0][:, 2 * h : 2 * h + 2, :])
-            pairs.append(pair)
-        rows = []
-        for j in range(PACK):
-            row = keep.tile([P, POOL], F32, name=f"row{j}")
-            nc.sync.dma_start(row[:], q_rows[1][:, j, :])
-            rows.append(row)
+        pair = keep.tile([P, 2, POOL], F32, name="pair")
+        nc.sync.dma_start(pair[:], q_rows[0][:, 0:2, :])
+        rows = {}
+        for o, j in ((0, 2), (1, 0), (0, 3), (1, 1), (1, 2), (1, 3)):
+            rows[o, j] = keep.tile([P, POOL], F32, name=f"row{o}{j}")
+            nc.sync.dma_start(rows[o, j][:], q_rows[o][:, j, :])
 
         scale_listed = keep.tile([P, B * N], U8, name="scale_listed", align_bytes=64)
         nc.vector.tensor_copy(scale_listed[:], scale_pool[:].indirect(key_list[:]))
@@ -78,12 +70,13 @@ def tile_attend_lq_wts_kernel(tc, qT, k_words, k_scales, offq, offs, out):
         woven = [keep.tile([P, B * NQ, PACK], BF16, name=f"woven{o}", align_bytes=64) for o in range(PASSES)]
         q_codes = [keep.tile([P, B * NQ], U32, name=f"q_codes{o}", align_bytes=64) for o in range(PASSES)]
         q_scales = [keep.tile([P, B * NQ], U8, name=f"q_scales{o}", align_bytes=64) for o in range(PASSES)]
+        cast = keep.tile([P, POOL, 2], BF16, name="cast")
+        nc.scalar.copy(cast[:], pair[:].rearrange("p j w -> p w j"))
+        pair_window = cast[:].rearrange("p w j -> p (w j)").bitcast(U32)
         woven_words = woven[0][:].rearrange("p n j -> p (n j)").bitcast(U32).rearrange("p (n h) -> p n h", h=2)
-        for h in range(2):
-            cast = keep.tile([P, POOL, 2], BF16, name=f"cast{h}")
-            nc.scalar.activation(cast[:], pairs[h][:].rearrange("p j w -> p w j"), ACT.Copy)
-            window = cast[:].rearrange("p w j -> p (w j)").bitcast(U32)
-            nc.vector.tensor_copy(woven_words[:, :, h], window.indirect(query_list[:]))
+        nc.vector.tensor_copy(woven_words[:, :, 0], pair_window.indirect(query_list[:]))
+        for j in range(2, PACK):
+            nc.vector.tensor_copy(woven[0][:, :, j], rows[0, j][:].indirect(query_list[:]))
         nc.vector.quantize_mx(
             out=q_codes[0][:].bitcast(FP8X4),
             scales=q_scales[0][:],
@@ -108,13 +101,16 @@ def tile_attend_lq_wts_kernel(tc, qT, k_words, k_scales, offq, offs, out):
         for b in range(B):
             multiply(b, 0)
 
-        for j in range(PACK - 1):
-            nc.vector.tensor_copy(woven[1][:, :, j], rows[j][:].indirect(query_list[:]))
+        for j in range(2):
+            rounded = keep.tile([P, POOL], BF16, name=f"rounded{j}")
+            nc.scalar.copy(rounded[:], rows[1, j][:])
+            nc.scalar.activation(woven[1][:, :, j], rounded[:].indirect(query_list[:]), ACT.Copy)
+        nc.vector.tensor_copy(woven[1][:, :, 2], rows[1, 2][:].indirect(query_list[:]))
         cols = NQ // 16
         for b in range(B):
             nc.vector.tensor_copy(
                 woven[1][:, b * NQ : (b + 1) * NQ, PACK - 1],
-                rows[PACK - 1][:].indirect(query_list[:, b * cols : (b + 1) * cols]),
+                rows[1, PACK - 1][:].indirect(query_list[:, b * cols : (b + 1) * cols]),
             )
         for b in range(B):
             qs = slice(b * NQ, (b + 1) * NQ)

@@ -38,25 +38,29 @@ def tile_attend_lq_wts_kernel(tc, qT, k_words, k_scales, offq, offs, out):
         nc.vector.memset(scale_pool[:].bitcast(I32), 0)
         nc.vector.memset(scale_late[:].bitcast(I32), 0)
 
+        q_rows = qT.rearrange("(o p j) w -> o p j w", o=PASSES, j=PACK)
+        rows = {}
+
+        def load_row(o, j):
+            rows[o, j] = keep.tile([P, POOL], F32, name=f"row{o}{j}")
+            nc.sync.dma_start(rows[o, j][:], q_rows[o][:, j, :])
+
         nc.sync.dma_start(key_list[:], offs)
+        load_row(0, 0)
+        nc.sync.dma_start(query_list[:], offq)
         nc.sync.dma_start(word_pool[:], k_words[0].rearrange("p t c -> p (t c)").bitcast(I32))
 
         scale_rows = k_scales.rearrange("o (q r) t -> r q o t", r=4)
         for r in range(4):
             nc.scalar.dma_start(scale_pool[r:P:SHIFT, :].bitcast(I32), scale_rows[r].bitcast(I32))
-        nc.sync.dma_start(query_list[:], offq)
 
-        q_rows = qT.rearrange("(o p j) w -> o p j w", o=PASSES, j=PACK)
-        pair = keep.tile([P, 2, POOL], F32, name="pair")
-        nc.sync.dma_start(pair[:], q_rows[0][:, 0:2, :])
-        rows = {}
-        for o, j in ((0, 2), (1, 0), (0, 3), (1, 1), (1, 2), (1, 3)):
-            rows[o, j] = keep.tile([P, POOL], F32, name=f"row{o}{j}")
-            nc.sync.dma_start(rows[o, j][:], q_rows[o][:, j, :])
+        for o, j in ((0, 1), (1, 0), (1, 1), (0, 2), (0, 3), (1, 2), (1, 3)):
+            load_row(o, j)
 
         scale_listed = keep.tile([P, B * N], U8, name="scale_listed", align_bytes=64)
         nc.vector.tensor_copy(scale_listed[:], scale_pool[:].indirect(key_list[:]))
-        nc.sync.dma_start(scale_late[0 : P - SHIFT, :].bitcast(I32), scale_listed[SHIFT:P, :].bitcast(I32))
+        for r in range(4):
+            nc.sync.dma_start(scale_late[r:P:32, :].bitcast(I32), scale_listed[SHIFT + r : P : 32, :].bitcast(I32))
         words_listed = keep.tile([P, B * N], U32, name="words_listed")
         nc.vector.tensor_copy(words_listed[:], word_pool[:].bitcast(U32).indirect(key_list[:]))
         halves = words_listed[:].bitcast(U16).rearrange("p (n h) -> p h n", h=2)
@@ -70,11 +74,11 @@ def tile_attend_lq_wts_kernel(tc, qT, k_words, k_scales, offq, offs, out):
         woven = [keep.tile([P, B * NQ, PACK], BF16, name=f"woven{o}", align_bytes=64) for o in range(PASSES)]
         q_codes = [keep.tile([P, B * NQ], U32, name=f"q_codes{o}", align_bytes=64) for o in range(PASSES)]
         q_scales = [keep.tile([P, B * NQ], U8, name=f"q_scales{o}", align_bytes=64) for o in range(PASSES)]
-        cast = keep.tile([P, POOL, 2], BF16, name="cast")
-        nc.scalar.copy(cast[:], pair[:].rearrange("p j w -> p w j"))
-        pair_window = cast[:].rearrange("p w j -> p (w j)").bitcast(U32)
-        woven_words = woven[0][:].rearrange("p n j -> p (n j)").bitcast(U32).rearrange("p (n h) -> p n h", h=2)
-        nc.vector.tensor_copy(woven_words[:, :, 0], pair_window.indirect(query_list[:]))
+        for o in range(PASSES):
+            for j in range(2):
+                rounded = keep.tile([P, POOL], BF16, name=f"rounded{o}{j}")
+                nc.scalar.copy(rounded[:], rows[o, j][:])
+                nc.scalar.activation(woven[o][:, :, j], rounded[:].indirect(query_list[:]), ACT.Copy)
         for j in range(2, PACK):
             nc.vector.tensor_copy(woven[0][:, :, j], rows[0, j][:].indirect(query_list[:]))
         nc.vector.quantize_mx(
@@ -101,10 +105,6 @@ def tile_attend_lq_wts_kernel(tc, qT, k_words, k_scales, offq, offs, out):
         for b in range(B):
             multiply(b, 0)
 
-        for j in range(2):
-            rounded = keep.tile([P, POOL], BF16, name=f"rounded{j}")
-            nc.scalar.copy(rounded[:], rows[1, j][:])
-            nc.scalar.activation(woven[1][:, :, j], rounded[:].indirect(query_list[:]), ACT.Copy)
         nc.vector.tensor_copy(woven[1][:, :, 2], rows[1, 2][:].indirect(query_list[:]))
         cols = NQ // 16
         for b in range(B):

from contextlib import ExitStack

import concourse.mybir as mybir

B, N, T, D, NQ, POOL = 2, 512, 2048, 1024, 128, 1024
FLOPS = 2 * B * NQ * N * D

F32 = mybir.dt.float32
BF16 = mybir.dt.bfloat16
I32 = mybir.dt.int32
U32 = mybir.dt.uint32
U16 = mybir.dt.uint16
U8 = mybir.dt.uint8
FP8X4 = mybir.dt.float8_e4m3fn_x4
FP4X4 = mybir.dt.float4_e2m1fn_x4
ACT = mybir.ActivationFunctionType
ALU = mybir.AluOpType
AX = mybir.AxisListType

P = 128
PACK = 4
PASSES = D // (P * PACK)
SHIFT = 16


def tile_attend_lq_wts_kernel(tc, qT, k_words, k_scales, offq, offs, out):
    nc = tc.nc
    with ExitStack() as ctx:
        keep = ctx.enter_context(tc.tile_pool(name="keep", bufs=1))
        psum = ctx.enter_context(tc.psum_pool(name="psum", bufs=1))

        key_list = keep.tile([P, B * N // 16], U16, name="key_list")
        query_list = keep.tile([P, B * NQ // 16], U16, name="query_list")
        word_pool = keep.tile([P, T], I32, name="word_pool")
        scale_pool = keep.tile([P, T], U8, name="scale_pool")
        scale_late = keep.tile([P, B * N], U8, name="scale_late", align_bytes=64)

        nc.vector.memset(scale_pool[:].bitcast(I32), 0)
        nc.vector.memset(scale_late[:].bitcast(I32), 0)

        q_rows = qT.rearrange("(o p j) w -> o p j w", o=PASSES, j=PACK)
        rows = {}

        def load_row(o, j):
            rows[o, j] = keep.tile([P, POOL], F32, name=f"row{o}{j}")
            nc.sync.dma_start(rows[o, j][:], q_rows[o][:, j, :])

        nc.sync.dma_start(key_list[:], offs)
        load_row(0, 0)
        nc.sync.dma_start(query_list[:], offq)
        nc.sync.dma_start(word_pool[:], k_words[0].rearrange("p t c -> p (t c)").bitcast(I32))

        scale_rows = k_scales.rearrange("o (q r) t -> r q o t", r=4)
        for r in range(4):
            nc.scalar.dma_start(scale_pool[r:P:SHIFT, :].bitcast(I32), scale_rows[r].bitcast(I32))

        for o, j in ((0, 1), (1, 0), (1, 1), (0, 2), (0, 3), (1, 2), (1, 3)):
            load_row(o, j)

        scale_listed = keep.tile([P, B * N], U8, name="scale_listed", align_bytes=64)
        nc.vector.tensor_copy(scale_listed[:], scale_pool[:].indirect(key_list[:]))
        for r in range(4):
            nc.sync.dma_start(scale_late[r:P:32, :].bitcast(I32), scale_listed[SHIFT + r : P : 32, :].bitcast(I32))
        words_listed = keep.tile([P, B * N], U32, name="words_listed")
        nc.vector.tensor_copy(words_listed[:], word_pool[:].bitcast(U32).indirect(key_list[:]))
        halves = words_listed[:].bitcast(U16).rearrange("p (n h) -> p h n", h=2)
        key_codes = []
        for o in range(PASSES):
            codes = keep.tile([P, B * N], U16, name=f"key_codes{o}", align_bytes=64)
            nc.vector.tensor_copy(codes[:], halves[:, o, :])
            key_codes.append(codes)
        key_scales = [scale_listed, scale_late]

        woven = [keep.tile([P, B * NQ, PACK], BF16, name=f"woven{o}", align_bytes=64) for o in range(PASSES)]
        q_codes = [keep.tile([P, B * NQ], U32, name=f"q_codes{o}", align_bytes=64) for o in range(PASSES)]
        q_scales = [keep.tile([P, B * NQ], U8, name=f"q_scales{o}", align_bytes=64) for o in range(PASSES)]
        for o in range(PASSES):
            for j in range(2):
                rounded = keep.tile([P, POOL], BF16, name=f"rounded{o}{j}")
                nc.scalar.copy(rounded[:], rows[o, j][:])
                nc.scalar.activation(woven[o][:, :, j], rounded[:].indirect(query_list[:]), ACT.Copy)
        for j in range(2, PACK):
            nc.vector.tensor_copy(woven[0][:, :, j], rows[0, j][:].indirect(query_list[:]))
        nc.vector.quantize_mx(
            out=q_codes[0][:].bitcast(FP8X4),
            scales=q_scales[0][:],
            in_=woven[0][:].rearrange("p n j -> p (n j)"),
        )

        scores = [psum.tile([P, N], F32, name=f"scores{b}") for b in range(B)]

        def multiply(b, o):
            qs = slice(b * NQ, (b + 1) * NQ)
            ks = slice(b * N, (b + 1) * N)
            nc.tensor.matmul_mx(
                out=scores[b][:],
                lhsT=q_codes[o][:, qs].bitcast(FP8X4),
                lhsT_scale=q_scales[o][:, qs],
                rhs=key_codes[o][:, ks].bitcast(FP4X4),
                rhs_scale=key_scales[o][:, ks],
                start=(o == 0),
                stop=(o == PASSES - 1),
            )

        for b in range(B):
            multiply(b, 0)

        nc.vector.tensor_copy(woven[1][:, :, 2], rows[1, 2][:].indirect(query_list[:]))
        cols = NQ // 16
        for b in range(B):
            nc.vector.tensor_copy(
                woven[1][:, b * NQ : (b + 1) * NQ, PACK - 1],
                rows[1, PACK - 1][:].indirect(query_list[:, b * cols : (b + 1) * cols]),
            )
        for b in range(B):
            qs = slice(b * NQ, (b + 1) * NQ)
            nc.vector.quantize_mx(
                out=q_codes[1][:, qs].bitcast(FP8X4),
                scales=q_scales[1][:, qs],
                in_=woven[1][:, qs, :].rearrange("p n j -> p (n j)"),
            )
            multiply(b, 1)

        neg_max = [keep.tile([P, 1], F32, name=f"neg_max{b}") for b in range(B)]
        total = [keep.tile([P, 1], F32, name=f"total{b}") for b in range(B)]
        inverse = [keep.tile([P, 1], F32, name=f"inverse{b}") for b in range(B)]
        weights = [keep.tile([P, N], F32, name=f"weights{b}") for b in range(B)]
        result = [keep.tile([P, N], F32, name=f"result{b}") for b in range(B)]
        for b in range(B):
            nc.vector.tensor_reduce(neg_max[b][:], scores[b][:], AX.X, ALU.max, negate=True)
            nc.scalar.activation(weights[b][:], scores[b][:], ACT.Exp, bias=neg_max[b][:], scale=1.0, accum_out=total[b][:])
        for b in range(B):
            nc.vector.reciprocal(inverse[b][:], total[b][:])
            nc.vector.tensor_scalar_mul(result[b][:], weights[b][:], inverse[b][:])
            nc.sync.dma_start(out[b], result[b][:])
